import numpy as np
import ml_dtypes


def mxq(x, axis, fmt="e4m3"):
    dtype, down = {"e4m3": (ml_dtypes.float8_e4m3fn, 7), "e5m2": (ml_dtypes.float8_e5m2, 14)}[fmt]
    v = np.moveaxis(np.asarray(x, np.float32).astype(ml_dtypes.bfloat16).astype(np.float64), axis, -1)
    blocks = v.reshape(v.shape[:-1] + (-1, 32))
    amax = np.abs(blocks).max(-1, keepdims=True)
    byte = np.maximum(np.where(amax > 0, np.frexp(amax)[1] - 1 + 127, 0) - down, 1)
    scale = np.exp2(byte - 127.0)
    codes = (blocks / scale).astype(np.float32).astype(dtype).astype(np.float64)
    return np.moveaxis((codes * scale).reshape(v.shape), -1, axis)


WIDE = False


def mx_kscale(k):
    if not WIDE:
        return np.ones(k)
    levels = np.array([10, -10, 5, -5, 0])
    if k % 512:
        return np.exp2(np.random.permutation(np.resize(levels, k // 32))).repeat(32)
    a = np.empty((k // 512, 16))
    for p in range(k // 512):
        a[p, :8] = np.random.permutation(np.resize(levels, 8))
        for g in range(8):
            far = levels[np.abs(levels - a[p, g]) >= 10]
            a[p, g + 8] = far[np.random.randint(len(far))]
    return np.exp2(a.ravel()).repeat(32)


def f64(x):
    return np.asarray(x).astype(np.float64)


def striped8(idx):
    return np.asarray(idx).reshape(8, -1, 16).transpose(0, 2, 1).reshape(128, -1).astype(np.uint16)


def unstriped8(offs):
    return offs.reshape(8, 16, -1).transpose(0, 2, 1).reshape(8, -1).astype(np.int64)


def pick8(x, idx, run):
    r = np.arange(len(x))
    return x[r[:, None], idx[r % (8 * run) // run]]


E2M1 = np.array([0.0, 0.5, 1.0, 1.5, 2.0, 3.0, 4.0, 6.0, -0.0, -0.5, -1.0, -1.5, -2.0, -3.0, -4.0, -6.0])


def pack_weight(w, fmt):
    k, n = w.shape
    w = f64(np.asarray(w, np.float32).astype(ml_dtypes.bfloat16)).reshape(k // 32, 32, n)
    amax = np.abs(w).max(1)
    if fmt == "e4m3":
        byte = np.frexp(amax)[1] - 1 + 127 - 7
    else:
        mant, ex = np.frexp(amax / 6.0)
        byte = np.where(mant > 0.5, ex, ex - 1) + 127
    byte = np.clip(np.where(amax > 0, byte, 1), 1, 254)
    scaled = (w * np.exp2(127.0 - byte)[:, None, :]).reshape(k, n).astype(np.float32)
    by_word = np.ascontiguousarray(scaled.reshape(k // 512, 128, 4, n).transpose(0, 1, 3, 2))
    if fmt == "e4m3":
        words = by_word.astype(ml_dtypes.float8_e4m3fn).view(np.uint8)
    else:
        c = by_word.astype(ml_dtypes.float4_e2m1fn).view(np.uint8) & 0xF
        words = (c[..., 0::2] | (c[..., 1::2] << 4)).reshape(k // 512, 128, 2 * n)
    return np.ascontiguousarray(words), np.ascontiguousarray(byte.astype(np.uint8).reshape(k // 512, 16, n))


def unpack_weight(words, scales, fmt):
    g, _, n = scales.shape
    words = np.ascontiguousarray(words).reshape(g, 128, n, -1)
    if fmt == "e4m3":
        vals = words.view(ml_dtypes.float8_e4m3fn).astype(np.float64)
    else:
        nib = np.empty((g, 128, n, 4), np.uint8)
        nib[..., 0::2] = words & 0xF
        nib[..., 1::2] = words >> 4
        vals = E2M1[nib]
    vals = vals * np.repeat(np.exp2(scales.astype(np.float64) - 127.0), 8, axis=1)[..., None]
    return vals.transpose(0, 1, 3, 2).reshape(g * 512, n)


def sigmoid(v):
    return 1.0 / (1.0 + np.exp(-v))


D, T, I, Q = 512, 1024, 512, 128


def setup_inputs():
    n = np.random.standard_normal
    idx = np.stack([np.random.permutation(T)[:I] for _ in range(8)])
    idx2 = np.stack([np.random.permutation(T)[:I] for _ in range(8)])
    idx3 = np.stack([np.random.permutation(T)[:I] for _ in range(8)])
    fd = mx_kscale(D)
    keysp = pack_weight(n((D, T)) / fd[:, None], "e4m3")
    return {
        "query": (n((D, Q)) * 1.0 / np.sqrt(D) * fd[:, None]).astype(np.float32),
        "keys_words": keysp[0],
        "keys_scales": keysp[1],
        "old": (1.0 * n((Q, T))).astype(np.float32),
        "offs": striped8(idx),
        "offs2": striped8(idx2),
        "offs3": striped8(idx3),
    }


def reference(query, keys_words, keys_scales, old, offs, offs2, offs3):
    idx = unstriped8(offs)
    idx2 = unstriped8(offs2)
    idx3 = unstriped8(offs3)
    keysu = unpack_weight(keys_words, keys_scales, "e4m3")
    queryq = mxq(f64(query), 0, "e4m3")
    a = queryq.T @ keysu
    s = pick8(a, idx, 16) - pick8(a, idx2, 16)
    w = sigmoid(s)
    f1 = np.zeros((Q, T))
    f1[np.arange(Q)[:, None], idx[np.arange(Q) % 128 // 16]] = w
    f2 = f1 + f64(old)
    y = pick8(f2, idx3, 16)
    return y

@@ -1,0 +1,121 @@
+from contextlib import ExitStack
+
+import concourse.mybir as mybir
+
+F32 = mybir.dt.float32
+BF16 = mybir.dt.bfloat16
+I32 = mybir.dt.int32
+U32 = mybir.dt.uint32
+U16 = mybir.dt.uint16
+U8 = mybir.dt.uint8
+FP8X4 = mybir.dt.float8_e4m3fn_x4
+ACT = mybir.ActivationFunctionType
+ALU = mybir.AluOpType
+
+P = 128
+D, T, I, Q = 512, 1024, 512, 128
+PACK = 4
+CHUNKS = 4
+N = T // CHUNKS
+HALF = I // 2
+HC = HALF // 16
+PIECES = [(0, 256), (256, 256), (512, 256), (768, 128), (896, 128)]
+RUNS = [(0, 128), (128, 384)]
+FLOPS = 2 * D * Q * T
+
+
+def tile_attend_difference_lean_through_heads_kernel(tc, query, keys_words, keys_scales, old, offs, offs2, offs3, out):
+    nc = tc.nc
+    with ExitStack() as ctx:
+        sb = ctx.enter_context(tc.tile_pool(name="sb", bufs=1))
+        ps = ctx.enter_context(tc.psum_pool(name="ps", bufs=1))
+
+        list1 = sb.tile([P, I // 16], U16, name="list1")
+        list2 = sb.tile([P, I // 16], U16, name="list2")
+        list3 = sb.tile([P, I // 16], U16, name="list3")
+        q_raw = sb.tile([P, PACK, Q], F32, name="q_raw")
+        q_bf = sb.tile([P, Q, PACK], BF16, name="q_bf", align_bytes=64)
+        q_codes = sb.tile([P, Q], U32, name="q_codes", align_bytes=64)
+        q_scale = sb.tile([P, Q], U8, name="q_scale", align_bytes=64)
+        k_codes = [sb.tile([P, T // 2], U32, name="k_codes%d" % h, align_bytes=64) for h in range(2)]
+        k_scale = sb.tile([P, N], U8, name="k_scale", align_bytes=64)
+        old_sb = sb.tile([P, T], F32, name="old_sb")
+        a = sb.tile([P, T], F32, name="a")
+        f1 = sb.tile([P, T], F32, name="f1")
+        f2 = sb.tile([P, T], F32, name="f2")
+        g1 = sb.tile([P, I], F32, name="g1")
+        g2 = sb.tile([P, I], F32, name="g2")
+        s = sb.tile([P, I], F32, name="s")
+        w = sb.tile([P, I], F32, name="w")
+        y = [sb.tile([P, HALF], F32, name="y_%d" % h) for h in range(2)]
+        banks = [ps.tile([P, n], F32, name="bank%d" % t0) for t0, n in PIECES]
+
+        nc.vector.memset(k_scale[:].bitcast(I32), 0)
+        warm_in = sb.tile([P, 1], F32, name="warm_in")
+        warm_out = sb.tile([P, 1], F32, name="warm_out")
+        nc.vector.memset(warm_in[:], 0.0)
+        nc.vector.memset(f1[:], 0.0)
+
+        words = keys_words[0].rearrange("p n t -> p (n t)")
+        scale_rows = keys_scales[0].rearrange("f (j c) -> j f c", j=CHUNKS)
+        nc.sync.dma_start(out=q_raw[:], in_=query.rearrange("(p t) q -> p t q", t=PACK))
+        for quad in range(4):
+            nc.sync.dma_start(
+                out=k_scale[32 * quad : 32 * quad + 16, :].bitcast(I32),
+                in_=scale_rows[:, 4 * quad : 4 * quad + 4, :].bitcast(I32),
+            )
+        for h in range(2):
+            nc.sync.dma_start(out=k_codes[h][:].bitcast(I32), in_=words[:, h * 2 * T : (h + 1) * 2 * T].bitcast(I32))
+        nc.sync.dma_start(list2[:], offs2)
+        nc.sync.dma_start(list1[:], offs)
+        nc.sync.dma_start(out=old_sb[:], in_=old)
+        nc.sync.dma_start(list3[:], offs3)
+        nc.scalar.activation(warm_out[:], warm_in[:], ACT.Sigmoid)
+
+        for h in range(2):
+            cols = slice(h * Q // 2, (h + 1) * Q // 2)
+            nc.vector.tensor_copy(out=q_bf[:, cols, :], in_=q_raw[:, :, cols].rearrange("p t q -> p q t"))
+        for h in range(2):
+            cols = slice(h * Q // 2, (h + 1) * Q // 2)
+            nc.vector.quantize_mx(
+                out=q_codes[:, cols].bitcast(FP8X4),
+                scales=q_scale[:, cols],
+                in_=q_bf[:, cols, :].rearrange("p q t -> p (q t)"),
+            )
+
+        for b, (t0, n) in enumerate(PIECES):
+            j, c = divmod(t0, N)
+            c0 = t0 % (T // 2)
+            nc.tensor.matmul_mx(
+                out=banks[b][:],
+                lhsT=q_codes[:].bitcast(FP8X4),
+                lhsT_scale=q_scale[:],
+                rhs=k_codes[j // 2][:, c0 : c0 + n].bitcast(FP8X4),
+                rhs_scale=k_scale[4 * j : P, c : c + n],
+                start=True,
+                stop=True,
+            )
+            if b % 2 == 0:
+                nc.scalar.copy(a[:, t0 : t0 + n], banks[b][:])
+            else:
+                nc.vector.tensor_copy(a[:, t0 : t0 + n], banks[b][:])
+
+        def piece(lst, h):
+            return lst[:, h * HC : (h + 1) * HC]
+
+        for h in range(2):
+            cols = slice(h * HALF, (h + 1) * HALF)
+            nc.vector.tensor_copy(g2[:, cols], a[:].indirect(piece(list2, h)))
+            nc.scalar.activation(g1[:, cols], a[:].indirect(piece(list1, h)), ACT.Copy)
+        for i0, n in RUNS:
+            cols = slice(i0, i0 + n)
+            nc.vector.tensor_tensor(s[:, cols], g1[:, cols], g2[:, cols], ALU.subtract)
+            nc.scalar.activation(w[:, cols], s[:, cols], ACT.Sigmoid)
+        for i0, n in RUNS:
+            nc.vector.tensor_copy(f1[:].indirect(list1[:, i0 // 16 : (i0 + n) // 16]), w[:, i0 : i0 + n])
+
+        nc.vector.tensor_tensor(f2[:], f1[:], old_sb[:], ALU.add)
+        nc.vector.tensor_copy(y[0][:], f2[:].indirect(piece(list3, 0)))
+        nc.scalar.activation(y[1][:], f2[:].indirect(piece(list3, 1)), ACT.Copy)
+        nc.sync.dma_start(out=out[:, 0:HALF], in_=y[0][:])
+        nc.scalar.dma_start(out=out[:, HALF:I], in_=y[1][:])

@@ -1,6 +1,7 @@
 from contextlib import ExitStack
 
 import concourse.mybir as mybir
+from concourse.masks import make_identity
 
 F32 = mybir.dt.float32
 BF16 = mybir.dt.bfloat16
@@ -45,27 +46,30 @@ def tile_attend_difference_lean_through_heads_kernel(tc, query, keys_words, keys
         f2 = sb.tile([P, T], F32, name="f2")
         g1 = sb.tile([P, I], F32, name="g1")
         g2 = sb.tile([P, I], F32, name="g2")
-        s = sb.tile([P, I], F32, name="s")
+        s = sb.tile([P, I], F32, name="s", tag="s")
         w = sb.tile([P, I], F32, name="w")
         y = [sb.tile([P, HALF], F32, name="y_%d" % h) for h in range(2)]
-        banks = [ps.tile([P, n], F32, name="bank%d" % t0) for t0, n in PIECES]
+        banks = [ps.tile([P, n], F32, name="bank%d" % t0, tag="bank%d" % t0) for t0, n in PIECES]
 
         nc.vector.memset(k_scale[:].bitcast(I32), 0)
         warm_in = sb.tile([P, 1], F32, name="warm_in")
         warm_out = sb.tile([P, 1], F32, name="warm_out")
         nc.vector.memset(warm_in[:], 0.0)
         nc.vector.memset(f1[:], 0.0)
+        ident = sb.tile([P, P], F32, name="ident")
+        nc.vector.memset(ident[:], 0.0)
+        make_identity(nc, ident[:], nomemset=True)
 
         words = keys_words[0].rearrange("p n t -> p (n t)")
         scale_rows = keys_scales[0].rearrange("f (j c) -> j f c", j=CHUNKS)
         nc.sync.dma_start(out=q_raw[:], in_=query.rearrange("(p t) q -> p t q", t=PACK))
+        nc.sync.dma_start(out=k_codes[0][:].bitcast(I32), in_=words[:, 0 : 2 * T].bitcast(I32))
         for quad in range(4):
             nc.sync.dma_start(
                 out=k_scale[32 * quad : 32 * quad + 16, :].bitcast(I32),
                 in_=scale_rows[:, 4 * quad : 4 * quad + 4, :].bitcast(I32),
             )
-        for h in range(2):
-            nc.sync.dma_start(out=k_codes[h][:].bitcast(I32), in_=words[:, h * 2 * T : (h + 1) * 2 * T].bitcast(I32))
+        nc.sync.dma_start(out=k_codes[1][:].bitcast(I32), in_=words[:, 2 * T : 4 * T].bitcast(I32))
         nc.sync.dma_start(list2[:], offs2)
         nc.sync.dma_start(list1[:], offs)
         nc.sync.dma_start(out=old_sb[:], in_=old)
@@ -111,10 +115,25 @@ def tile_attend_difference_lean_through_heads_kernel(tc, query, keys_words, keys
             cols = slice(i0, i0 + n)
             nc.vector.tensor_tensor(s[:, cols], g1[:, cols], g2[:, cols], ALU.subtract)
             nc.scalar.activation(w[:, cols], s[:, cols], ACT.Sigmoid)
+        spans = [(0, 512), (512, 128)]
+        old_t = sb.tile([P, 640], F32, name="old_t", tag="s")
+        old_ps = []
+        for b, (t0, n) in enumerate(spans):
+            turned = ps.tile([P, n], F32, name="turned%d" % b, tag="bank%d" % PIECES[b][0])
+            for c in range(0, n, P):
+                nc.tensor.transpose(turned[:, c : c + P], old_sb[:, t0 + c : t0 + c + P], ident[:])
+            nc.scalar.copy(old_t[:, t0 : t0 + n], turned[:])
+        for b, (t0, n) in enumerate(spans):
+            back = ps.tile([P, n], F32, name="back%d" % b)
+            for c in range(0, n, P):
+                nc.tensor.transpose(back[:, c : c + P], old_t[:, t0 + c : t0 + c + P], ident[:])
+            old_ps.append(back)
         for i0, n in RUNS:
             nc.vector.tensor_copy(f1[:].indirect(list1[:, i0 // 16 : (i0 + n) // 16]), w[:, i0 : i0 + n])
 
-        nc.vector.tensor_tensor(f2[:], f1[:], old_sb[:], ALU.add)
+        nc.gpsimd.tensor_tensor(f2[:, 640:T], f1[:, 640:T], old_sb[:, 640:T], ALU.add)
+        for b, (t0, n) in enumerate(spans):
+            nc.vector.tensor_tensor(f2[:, t0 : t0 + n], f1[:, t0 : t0 + n], old_ps[b][:], ALU.add)
         nc.vector.tensor_copy(y[0][:], f2[:].indirect(piece(list3, 0)))
         nc.scalar.activation(y[1][:], f2[:].indirect(piece(list3, 1)), ACT.Copy)
         nc.sync.dma_start(out=out[:, 0:HALF], in_=y[0][:])

@@ -43,6 +43,8 @@ def tile_attend_difference_lean_through_heads_kernel(tc, query, keys_words, keys
         old_sb = sb.tile([P, T], F32, name="old_sb")
         a = sb.tile([P, T], F32, name="a")
         f1 = sb.tile([P, T], F32, name="f1")
+        f0 = sb.tile([P, T], F32, name="f0")
+        part = sb.tile([P, T - 640], F32, name="part")
         f2 = sb.tile([P, T], F32, name="f2")
         g1 = sb.tile([P, I], F32, name="g1")
         g2 = sb.tile([P, I], F32, name="g2")
@@ -55,10 +57,11 @@ def tile_attend_difference_lean_through_heads_kernel(tc, query, keys_words, keys
         warm_in = sb.tile([P, 1], F32, name="warm_in")
         warm_out = sb.tile([P, 1], F32, name="warm_out")
         nc.vector.memset(warm_in[:], 0.0)
-        nc.vector.memset(f1[:], 0.0)
         ident = sb.tile([P, P], F32, name="ident")
         nc.vector.memset(ident[:], 0.0)
         make_identity(nc, ident[:], nomemset=True)
+        nc.vector.memset(f0[:], 0.0)
+        nc.vector.memset(f1[:], 0.0)
 
         words = keys_words[0].rearrange("p n t -> p (n t)")
         scale_rows = keys_scales[0].rearrange("f (j c) -> j f c", j=CHUNKS)
@@ -111,29 +114,28 @@ def tile_attend_difference_lean_through_heads_kernel(tc, query, keys_words, keys
             cols = slice(h * HALF, (h + 1) * HALF)
             nc.vector.tensor_copy(g2[:, cols], a[:].indirect(piece(list2, h)))
             nc.scalar.activation(g1[:, cols], a[:].indirect(piece(list1, h)), ACT.Copy)
-        for i0, n in RUNS:
+        for i0, n in [(0, 128), (128, 128), (256, 256)]:
             cols = slice(i0, i0 + n)
             nc.vector.tensor_tensor(s[:, cols], g1[:, cols], g2[:, cols], ALU.subtract)
             nc.scalar.activation(w[:, cols], s[:, cols], ACT.Sigmoid)
         spans = [(0, 512), (512, 128)]
-        old_t = sb.tile([P, 640], F32, name="old_t", tag="s")
-        old_ps = []
-        for b, (t0, n) in enumerate(spans):
-            turned = ps.tile([P, n], F32, name="turned%d" % b, tag="bank%d" % PIECES[b][0])
-            for c in range(0, n, P):
-                nc.tensor.transpose(turned[:, c : c + P], old_sb[:, t0 + c : t0 + c + P], ident[:])
-            nc.scalar.copy(old_t[:, t0 : t0 + n], turned[:])
-        for b, (t0, n) in enumerate(spans):
-            back = ps.tile([P, n], F32, name="back%d" % b)
-            for c in range(0, n, P):
-                nc.tensor.transpose(back[:, c : c + P], old_t[:, t0 + c : t0 + c + P], ident[:])
-            old_ps.append(back)
-        for i0, n in RUNS:
-            nc.vector.tensor_copy(f1[:].indirect(list1[:, i0 // 16 : (i0 + n) // 16]), w[:, i0 : i0 + n])
+        old_t = sb.tile([P, 640], F32, name="old_t")
+        turned = [ps.tile([P, P], F32, name="turned%d" % b, tag="bank%d" % PIECES[b][0]) for b in range(5)]
+        back = [ps.tile([P, n], F32, name="back%d" % t0) for t0, n in spans]
+        for b in range(5):
+            nc.tensor.matmul(turned[b][:], old_sb[:, b * P : (b + 1) * P], ident[:], start=True, stop=False, is_transpose=True)
+        for dst, (i0, n) in zip((f0, f1), RUNS):
+            nc.vector.tensor_copy(dst[:].indirect(list1[:, i0 // 16 : (i0 + n) // 16]), w[:, i0 : i0 + n])
+        nc.gpsimd.tensor_tensor(part[:], f0[:, 640:T], old_sb[:, 640:T], ALU.add)
+        for b in range(5):
+            nc.tensor.matmul(turned[b][:], f0[:, b * P : (b + 1) * P], ident[:], start=False, stop=True, is_transpose=True)
+            nc.scalar.copy(old_t[:, b * P : (b + 1) * P], turned[b][:])
+        for b in range(5):
+            nc.tensor.transpose(back[b // 4][:, (b % 4) * P : (b % 4 + 1) * P], old_t[:, b * P : (b + 1) * P], ident[:])
 
-        nc.gpsimd.tensor_tensor(f2[:, 640:T], f1[:, 640:T], old_sb[:, 640:T], ALU.add)
+        nc.gpsimd.tensor_tensor(f2[:, 640:T], f1[:, 640:T], part[:], ALU.add)
         for b, (t0, n) in enumerate(spans):
-            nc.vector.tensor_tensor(f2[:, t0 : t0 + n], f1[:, t0 : t0 + n], old_ps[b][:], ALU.add)
+            nc.vector.tensor_tensor(f2[:, t0 : t0 + n], f1[:, t0 : t0 + n], back[b][:], ALU.add)
         nc.vector.tensor_copy(y[0][:], f2[:].indirect(piece(list3, 0)))
         nc.scalar.activation(y[1][:], f2[:].indirect(piece(list3, 1)), ACT.Copy)
         nc.sync.dma_start(out=out[:, 0:HALF], in_=y[0][:])

from contextlib import ExitStack

import concourse.mybir as mybir
from concourse.masks import make_identity

F32 = mybir.dt.float32
BF16 = mybir.dt.bfloat16
I32 = mybir.dt.int32
U32 = mybir.dt.uint32
U16 = mybir.dt.uint16
U8 = mybir.dt.uint8
FP8X4 = mybir.dt.float8_e4m3fn_x4
ACT = mybir.ActivationFunctionType
ALU = mybir.AluOpType

P = 128
D, T, I, Q = 512, 1024, 512, 128
PACK = 4
CHUNKS = 4
N = T // CHUNKS
HALF = I // 2
HC = HALF // 16
PIECES = [(0, 256), (256, 256), (512, 256), (768, 128), (896, 128)]
RUNS = [(0, 128), (128, 384)]
FLOPS = 2 * D * Q * T


def tile_attend_difference_lean_through_heads_kernel(tc, query, keys_words, keys_scales, old, offs, offs2, offs3, out):
    nc = tc.nc
    with ExitStack() as ctx:
        sb = ctx.enter_context(tc.tile_pool(name="sb", bufs=1))
        ps = ctx.enter_context(tc.psum_pool(name="ps", bufs=1))

        list1 = sb.tile([P, I // 16], U16, name="list1")
        list2 = sb.tile([P, I // 16], U16, name="list2")
        list3 = sb.tile([P, I // 16], U16, name="list3")
        q_raw = sb.tile([P, PACK, Q], F32, name="q_raw")
        q_bf = sb.tile([P, Q, PACK], BF16, name="q_bf", align_bytes=64)
        q_codes = sb.tile([P, Q], U32, name="q_codes", align_bytes=64)
        q_scale = sb.tile([P, Q], U8, name="q_scale", align_bytes=64)
        k_codes = [sb.tile([P, T // 2], U32, name="k_codes%d" % h, align_bytes=64) for h in range(2)]
        k_scale = sb.tile([P, N], U8, name="k_scale", align_bytes=64)
        old_sb = sb.tile([P, T], F32, name="old_sb")
        a = sb.tile([P, T], F32, name="a")
        f1 = sb.tile([P, T], F32, name="f1")
        f0 = sb.tile([P, T], F32, name="f0")
        part = sb.tile([P, T - 640], F32, name="part")
        f2 = sb.tile([P, T], F32, name="f2")
        g1 = sb.tile([P, I], F32, name="g1")
        g2 = sb.tile([P, I], F32, name="g2")
        s = sb.tile([P, I], F32, name="s", tag="s")
        w = sb.tile([P, I], F32, name="w")
        y = [sb.tile([P, HALF], F32, name="y_%d" % h) for h in range(2)]
        banks = [ps.tile([P, n], F32, name="bank%d" % t0, tag="bank%d" % t0) for t0, n in PIECES]

        nc.vector.memset(k_scale[:].bitcast(I32), 0)
        warm_in = sb.tile([P, 1], F32, name="warm_in")
        warm_out = sb.tile([P, 1], F32, name="warm_out")
        nc.vector.memset(warm_in[:], 0.0)
        ident = sb.tile([P, P], F32, name="ident")
        nc.vector.memset(ident[:], 0.0)
        make_identity(nc, ident[:], nomemset=True)
        nc.vector.memset(f0[:], 0.0)
        nc.vector.memset(f1[:], 0.0)

        words = keys_words[0].rearrange("p n t -> p (n t)")
        scale_rows = keys_scales[0].rearrange("f (j c) -> j f c", j=CHUNKS)
        nc.sync.dma_start(out=q_raw[:], in_=query.rearrange("(p t) q -> p t q", t=PACK))
        nc.sync.dma_start(out=k_codes[0][:].bitcast(I32), in_=words[:, 0 : 2 * T].bitcast(I32))
        for quad in range(4):
            nc.sync.dma_start(
                out=k_scale[32 * quad : 32 * quad + 16, :].bitcast(I32),
                in_=scale_rows[:, 4 * quad : 4 * quad + 4, :].bitcast(I32),
            )
        nc.sync.dma_start(out=k_codes[1][:].bitcast(I32), in_=words[:, 2 * T : 4 * T].bitcast(I32))
        nc.sync.dma_start(list2[:], offs2)
        nc.sync.dma_start(list1[:], offs)
        nc.sync.dma_start(out=old_sb[:], in_=old)
        nc.sync.dma_start(list3[:], offs3)
        nc.scalar.activation(warm_out[:], warm_in[:], ACT.Sigmoid)

        for h in range(2):
            cols = slice(h * Q // 2, (h + 1) * Q // 2)
            nc.vector.tensor_copy(out=q_bf[:, cols, :], in_=q_raw[:, :, cols].rearrange("p t q -> p q t"))
        for h in range(2):
            cols = slice(h * Q // 2, (h + 1) * Q // 2)
            nc.vector.quantize_mx(
                out=q_codes[:, cols].bitcast(FP8X4),
                scales=q_scale[:, cols],
                in_=q_bf[:, cols, :].rearrange("p q t -> p (q t)"),
            )

        for b, (t0, n) in enumerate(PIECES):
            j, c = divmod(t0, N)
            c0 = t0 % (T // 2)
            nc.tensor.matmul_mx(
                out=banks[b][:],
                lhsT=q_codes[:].bitcast(FP8X4),
                lhsT_scale=q_scale[:],
                rhs=k_codes[j // 2][:, c0 : c0 + n].bitcast(FP8X4),
                rhs_scale=k_scale[4 * j : P, c : c + n],
                start=True,
                stop=True,
            )
            if b % 2 == 0:
                nc.scalar.copy(a[:, t0 : t0 + n], banks[b][:])
            else:
                nc.vector.tensor_copy(a[:, t0 : t0 + n], banks[b][:])

        def piece(lst, h):
            return lst[:, h * HC : (h + 1) * HC]

        for h in range(2):
            cols = slice(h * HALF, (h + 1) * HALF)
            nc.vector.tensor_copy(g2[:, cols], a[:].indirect(piece(list2, h)))
            nc.scalar.activation(g1[:, cols], a[:].indirect(piece(list1, h)), ACT.Copy)
        for i0, n in [(0, 128), (128, 128), (256, 256)]:
            cols = slice(i0, i0 + n)
            nc.vector.tensor_tensor(s[:, cols], g1[:, cols], g2[:, cols], ALU.subtract)
            nc.scalar.activation(w[:, cols], s[:, cols], ACT.Sigmoid)
        spans = [(0, 512), (512, 128)]
        old_t = sb.tile([P, 640], F32, name="old_t")
        turned = [ps.tile([P, P], F32, name="turned%d" % b, tag="bank%d" % PIECES[b][0]) for b in range(5)]
        back = [ps.tile([P, n], F32, name="back%d" % t0) for t0, n in spans]
        for b in range(5):
            nc.tensor.matmul(turned[b][:], old_sb[:, b * P : (b + 1) * P], ident[:], start=True, stop=False, is_transpose=True)
        for dst, (i0, n) in zip((f0, f1), RUNS):
            nc.vector.tensor_copy(dst[:].indirect(list1[:, i0 // 16 : (i0 + n) // 16]), w[:, i0 : i0 + n])
        nc.gpsimd.tensor_tensor(part[:], f0[:, 640:T], old_sb[:, 640:T], ALU.add)
        for b in range(5):
            nc.tensor.matmul(turned[b][:], f0[:, b * P : (b + 1) * P], ident[:], start=False, stop=True, is_transpose=True)
            nc.scalar.copy(old_t[:, b * P : (b + 1) * P], turned[b][:])
        for b in range(5):
            nc.tensor.transpose(back[b // 4][:, (b % 4) * P : (b % 4 + 1) * P], old_t[:, b * P : (b + 1) * P], ident[:])

        nc.gpsimd.tensor_tensor(f2[:, 640:T], f1[:, 640:T], part[:], ALU.add)
        for b, (t0, n) in enumerate(spans):
            nc.vector.tensor_tensor(f2[:, t0 : t0 + n], f1[:, t0 : t0 + n], back[b][:], ALU.add)
        nc.vector.tensor_copy(y[0][:], f2[:].indirect(piece(list3, 0)))
        nc.scalar.activation(y[1][:], f2[:].indirect(piece(list3, 1)), ACT.Copy)
        nc.sync.dma_start(out=out[:, 0:HALF], in_=y[0][:])
        nc.scalar.dma_start(out=out[:, HALF:I], in_=y[1][:])
